import numpy as np
import ml_dtypes


def mxq(x, axis, fmt="e4m3"):
    dtype, down = {"e4m3": (ml_dtypes.float8_e4m3fn, 7), "e5m2": (ml_dtypes.float8_e5m2, 14)}[fmt]
    v = np.moveaxis(np.asarray(x, np.float32).astype(ml_dtypes.bfloat16).astype(np.float64), axis, -1)
    blocks = v.reshape(v.shape[:-1] + (-1, 32))
    amax = np.abs(blocks).max(-1, keepdims=True)
    byte = np.maximum(np.where(amax > 0, np.frexp(amax)[1] - 1 + 127, 0) - down, 1)
    scale = np.exp2(byte - 127.0)
    codes = (blocks / scale).astype(np.float32).astype(dtype).astype(np.float64)
    return np.moveaxis((codes * scale).reshape(v.shape), -1, axis)


WIDE = False


def mx_kscale(k):
    if not WIDE:
        return np.ones(k)
    levels = np.array([10, -10, 5, -5, 0])
    if k % 512:
        return np.exp2(np.random.permutation(np.resize(levels, k // 32))).repeat(32)
    a = np.empty((k // 512, 16))
    for p in range(k // 512):
        a[p, :8] = np.random.permutation(np.resize(levels, 8))
        for g in range(8):
            far = levels[np.abs(levels - a[p, g]) >= 10]
            a[p, g + 8] = far[np.random.randint(len(far))]
    return np.exp2(a.ravel()).repeat(32)


def f64(x):
    return np.asarray(x).astype(np.float64)


def striped(idx):
    return np.tile(np.asarray(idx).reshape(-1, 16).T, (8, 1)).astype(np.uint16)


def unstriped(offs):
    return offs[:16].T.reshape(-1).astype(np.int64)


E2M1 = np.array([0.0, 0.5, 1.0, 1.5, 2.0, 3.0, 4.0, 6.0, -0.0, -0.5, -1.0, -1.5, -2.0, -3.0, -4.0, -6.0])


def pack_weight(w, fmt):
    k, n = w.shape
    w = f64(np.asarray(w, np.float32).astype(ml_dtypes.bfloat16)).reshape(k // 32, 32, n)
    amax = np.abs(w).max(1)
    if fmt == "e4m3":
        byte = np.frexp(amax)[1] - 1 + 127 - 7
    else:
        mant, ex = np.frexp(amax / 6.0)
        byte = np.where(mant > 0.5, ex, ex - 1) + 127
    byte = np.clip(np.where(amax > 0, byte, 1), 1, 254)
    scaled = (w * np.exp2(127.0 - byte)[:, None, :]).reshape(k, n).astype(np.float32)
    by_word = np.ascontiguousarray(scaled.reshape(k // 512, 128, 4, n).transpose(0, 1, 3, 2))
    if fmt == "e4m3":
        words = by_word.astype(ml_dtypes.float8_e4m3fn).view(np.uint8)
    else:
        c = by_word.astype(ml_dtypes.float4_e2m1fn).view(np.uint8) & 0xF
        words = (c[..., 0::2] | (c[..., 1::2] << 4)).reshape(k // 512, 128, 2 * n)
    return np.ascontiguousarray(words), np.ascontiguousarray(byte.astype(np.uint8).reshape(k // 512, 16, n))


def unpack_weight(words, scales, fmt):
    g, _, n = scales.shape
    words = np.ascontiguousarray(words).reshape(g, 128, n, -1)
    if fmt == "e4m3":
        vals = words.view(ml_dtypes.float8_e4m3fn).astype(np.float64)
    else:
        nib = np.empty((g, 128, n, 4), np.uint8)
        nib[..., 0::2] = words & 0xF
        nib[..., 1::2] = words >> 4
        vals = E2M1[nib]
    vals = vals * np.repeat(np.exp2(scales.astype(np.float64) - 127.0), 8, axis=1)[..., None]
    return vals.transpose(0, 1, 3, 2).reshape(g * 512, n)


def bf(x):
    return np.asarray(x, np.float32).astype(ml_dtypes.bfloat16)


def planes(Y):
    r, m = Y.shape
    b = f64(bf(Y)).reshape(r // 32, 32, m)
    amax = np.abs(b).max(1)
    byte = np.clip(np.where(amax > 0, np.frexp(amax)[1] - 1 + 127 - 7, 1), 1, 254)
    codes = (b * np.exp2(127.0 - byte)[:, None, :]).reshape(r, m).astype(np.float32).astype(ml_dtypes.float8_e4m3fn).view(np.uint8)
    words = codes.reshape(r // 512, 128, 4, m).transpose(0, 1, 3, 2)
    return np.ascontiguousarray(words), np.ascontiguousarray(byte.astype(np.uint8).reshape(r // 512, 16, m))


K, T, J, N, L, R = 512, 1024, 512, 512, 512, 512


def setup_inputs():
    n = np.random.standard_normal
    idx = np.random.permutation(T)[:J]
    fk = mx_kscale(K)
    fr = mx_kscale(R)
    fl = mx_kscale(L)
    xtp = pack_weight(n((K, T)) / fk[:, None], "e2m1")
    wap = pack_weight(n((K, R)) * 1 / np.sqrt(K) * fk[:, None] * fr, "e4m3")
    wbp = pack_weight(n((R, N)) * 1 / np.sqrt(R) / fr[:, None], "e2m1")
    sxp = pack_weight(n((L, J)) / fl[:, None], "e4m3")
    wcp = pack_weight(n((L, N)) * 1 / np.sqrt(L) * fl[:, None], "e2m1")
    return {
        "xt_words": xtp[0],
        "xt_scales": xtp[1],
        "wa_words": wap[0],
        "wa_scales": wap[1],
        "wb_words": wbp[0],
        "wb_scales": wbp[1],
        "sx_words": sxp[0],
        "sx_scales": sxp[1],
        "wc_words": wcp[0],
        "wc_scales": wcp[1],
        "ga": (np.random.uniform(0.4, 1.2, (1, J))).astype(np.float32),
        "offs": striped(idx),
    }


def reference(xt_words, xt_scales, wa_words, wa_scales, wb_words, wb_scales, sx_words, sx_scales, wc_words, wc_scales, ga, offs):
    idx = unstriped(offs)
    xtu = unpack_weight(xt_words, xt_scales, "e2m1")
    wau = unpack_weight(wa_words, wa_scales, "e4m3")
    wbu = unpack_weight(wb_words, wb_scales, "e2m1")
    sxu = unpack_weight(sx_words, sx_scales, "e4m3")
    wcu = unpack_weight(wc_words, wc_scales, "e2m1")
    xtidxg = xtu[:, idx]
    a = wau.T @ xtidxg
    hid = np.maximum(a, 0.0)
    hidq = mxq(hid, 0, "e4m3")
    p = wbu.T @ hidq + wcu.T @ sxu
    pw = p * f64(ga)
    y = np.zeros((N, T))
    y[:, idx] = pw
    words, scales = planes(y)
    return y, words, scales

@@ -1,0 +1,193 @@
+from contextlib import ExitStack
+
+import concourse.mybir as mybir
+from concourse.masks import make_identity
+
+K, T, J, N, L, R = 512, 1024, 512, 512, 512, 512
+FLOPS = 2 * J * (K * R + R * N + L * N)
+
+F32 = mybir.dt.float32
+BF16 = mybir.dt.bfloat16
+I32 = mybir.dt.int32
+U16 = mybir.dt.uint16
+U8 = mybir.dt.uint8
+FP8X4 = mybir.dt.float8_e4m3fn_x4
+FP4X4 = mybir.dt.float4_e2m1fn_x4
+RELU = mybir.ActivationFunctionType.Relu
+MULT = mybir.AluOpType.mult
+
+P = 128
+PACK = 4
+CHUNK = 128
+CHUNKS = J // CHUNK
+HALF = T // 2
+
+
+def load_scale_rows(nc, plane, scales):
+    for r in range(4):
+        nc.sync.dma_start(out=plane[r:P:32, :].bitcast(I32), in_=scales[0, r:16:4, :].bitcast(I32))
+
+
+def deal_columns(nc, dealt, raw):
+    nc.vector.tensor_copy(
+        out=dealt.rearrange("p (t m) -> p t m", t=PACK),
+        in_=raw.rearrange("p (m t) -> p t m", t=PACK),
+    )
+
+
+def tile_moe_expert_hidden_and_given_pl_kernel(
+    tc, xt_words, xt_scales, wa_words, wa_scales, wb_words, wb_scales, sx_words, sx_scales, wc_words, wc_scales, ga, offs,
+    out_0, out_1, out_2,
+):
+    nc = tc.nc
+    with ExitStack() as ctx:
+        keep = ctx.enter_context(tc.tile_pool(name="keep", bufs=1))
+        psum = ctx.enter_context(tc.psum_pool(name="psum", bufs=1))
+
+        def sb(name, shape, dtype):
+            return keep.tile(shape, dtype, name=name, align_bytes=64)
+
+        offsets = keep.tile([P, J // 16], U16, name="offsets")
+        xw = sb("xw", [P, T], U16)
+        xs = sb("xs", [P, T], U8)
+        waw = sb("waw", [P, R], I32)
+        was = sb("was", [P, R], U8)
+        wbw = sb("wbw", [P, N], U16)
+        wbs = sb("wbs", [P, N], U8)
+        wcw = sb("wcw", [P, N], U16)
+        wcs = sb("wcs", [P, N], U8)
+        sxw = sb("sxw", [P, J], I32)
+        sxs = sb("sxs", [P, J], U8)
+        ga_cols = sb("ga_cols", [P, PACK], F32)
+        ident = sb("ident", [P, P], F32)
+        y = [sb("y%d" % t, [P, T], F32) for t in range(PACK)]
+
+        for plane in (was, xs, wbs, wcs, sxs):
+            nc.vector.memset(plane[:].bitcast(I32), 0)
+        make_identity(nc, ident[:])
+
+        nc.sync.dma_start(offsets[:], offs)
+        nc.sync.dma_start(out=xw[:].bitcast(I32), in_=xt_words[0].bitcast(I32))
+        nc.sync.dma_start(out=waw[:], in_=wa_words[0].rearrange("p c r -> p (c r)").bitcast(I32))
+        load_scale_rows(nc, was, wa_scales)
+        nc.sync.dma_start(out=ga_cols[:], in_=ga.rearrange("o (p c) -> p (o c)", c=PACK))
+        load_scale_rows(nc, xs, xt_scales)
+        nc.sync.dma_start(out=wbw[:].bitcast(I32), in_=wb_words[0].bitcast(I32))
+        load_scale_rows(nc, wbs, wb_scales)
+        nc.sync.dma_start(out=wcw[:].bitcast(I32), in_=wc_words[0].bitcast(I32))
+        load_scale_rows(nc, wcs, wc_scales)
+        nc.sync.dma_start(out=sxw[:], in_=sx_words[0].rearrange("p c r -> p (c r)").bitcast(I32))
+        load_scale_rows(nc, sxs, sx_scales)
+
+        xgw = sb("xgw", [P, J], U16)
+        xgs = sb("xgs", [P, J], U8)
+
+        def gather(lo, hi):
+            lst = offsets[:, lo // 16 : hi // 16]
+            nc.vector.tensor_copy(out=xgw[:, lo:hi], in_=xw[:].indirect(lst))
+            nc.vector.tensor_copy(out=xgs[:, lo:hi], in_=xs[:].indirect(lst))
+
+        waw_d = sb("waw_d", [P, R], I32)
+        was_d = sb("was_d", [P, R], U8)
+        wbw_d = sb("wbw_d", [P, N], U16)
+        wbs_d = sb("wbs_d", [P, N], U8)
+        wcw_d = sb("wcw_d", [P, N], U16)
+        wcs_d = sb("wcs_d", [P, N], U8)
+
+        gather(0, CHUNK)
+        deal_columns(nc, waw_d[:], waw[:])
+        deal_columns(nc, was_d[:], was[:])
+        gather(CHUNK, J)
+        deal_columns(nc, wbw_d[:], wbw[:])
+        deal_columns(nc, wbs_d[:], wbs[:])
+        deal_columns(nc, wcw_d[:], wcw[:])
+        deal_columns(nc, wcs_d[:], wcs[:])
+
+        for t in range(PACK):
+            (nc.vector if t < 2 else nc.gpsimd).memset(y[t][:], 0.0)
+
+        ga_ps = psum.tile([P, PACK, P], F32, name="ga_ps", tag="full3")
+        for c in range(PACK):
+            nc.tensor.transpose(ga_ps[:, c, :], ga_cols[:, c : c + 1].to_broadcast([P, P]), ident[:])
+        ga_all = sb("ga_all", [P, J], F32)
+        nc.scalar.copy(out=ga_all[:].rearrange("p (q c) -> p q c", c=PACK), in_=ga_ps[:].rearrange("p c q -> p q c"))
+
+        hid = sb("hid", [P, J * PACK], BF16)
+        hq = sb("hq", [P, J], I32)
+        hs = sb("hs", [P, J], U8)
+        psb = [sb("psb%d" % t, [P, J], F32) for t in range(PACK)]
+
+        def cols(i):
+            return slice(i * P, (i + 1) * P)
+
+        def given_pass(bank, t, js, first):
+            nc.tensor.matmul_mx(out=bank, lhsT=wcw_d[:, cols(t)].bitcast(FP4X4), lhsT_scale=wcs_d[:, cols(t)],
+                                rhs=sxw[:, js].bitcast(FP8X4), rhs_scale=sxs[:, js], start=first, stop=not first)
+
+        def hidden_pass(bank, t, js, first):
+            nc.tensor.matmul_mx(out=bank, lhsT=wbw_d[:, cols(t)].bitcast(FP4X4), lhsT_scale=wbs_d[:, cols(t)],
+                                rhs=hq[:, js].bitcast(FP8X4), rhs_scale=hs[:, js], start=first, stop=not first)
+
+        def second_layer(bank, t, js):
+            hidden_pass(bank, t, js, True)
+            given_pass(bank, t, js, False)
+
+        def scatter(t, js):
+            nc.vector.tensor_tensor(y[t][:].indirect(offsets[:, js.start // 16 : js.stop // 16]), psb[t][:, js], ga_all[:, js], MULT)
+
+        def first_layer(c):
+            a_ps = psum.tile([P, PACK, CHUNK], F32, name="a_ps", tag="a%d" % (c % 3))
+            for t in range(PACK):
+                nc.tensor.matmul_mx(out=a_ps[:, t, :], lhsT=waw_d[:, cols(t)].bitcast(FP8X4), lhsT_scale=was_d[:, cols(t)],
+                                    rhs=xgw[:, cols(c)].bitcast(FP4X4), rhs_scale=xgs[:, cols(c)], start=True, stop=True)
+            h = hid[:, c * CHUNK * PACK : (c + 1) * CHUNK * PACK]
+            nc.scalar.activation(out=h.rearrange("p (j t) -> p j t", t=PACK), in_=a_ps[:].rearrange("p t j -> p j t"), func=RELU)
+
+        def quantize_hidden(c):
+            nc.vector.quantize_mx(out=hq[:, cols(c)].bitcast(FP8X4), scales=hs[:, cols(c)],
+                                  in_=hid[:, c * CHUNK * PACK : (c + 1) * CHUNK * PACK])
+
+        def first_plane(c):
+            bank = psum.tile([P, CHUNK], F32, name="piece", tag="piece%d" % (c % 2))
+            second_layer(bank[:], 0, cols(c))
+            nc.scalar.copy(out=psb[0][:, cols(c)], in_=bank[:])
+            scatter(0, cols(c))
+
+        first_layer(0)
+        for c in range(CHUNKS):
+            if c + 1 < CHUNKS:
+                first_layer(c + 1)
+            quantize_hidden(c)
+            if c > 0:
+                first_plane(c - 1)
+        first_plane(CHUNKS - 1)
+        for t in range(1, PACK):
+            bank = psum.tile([P, J], F32, name="full", tag="full%d" % t)
+            second_layer(bank[:], t, slice(0, J))
+            nc.scalar.copy(out=psb[t][:], in_=bank[:])
+
+        grouped = sb("grouped", [P, T, PACK], BF16)
+        yq = sb("yq", [P, T], I32)
+        ys = sb("ys", [P, T], U8)
+        rows = out_0.rearrange("(p t) c -> t p c", t=PACK)
+        lo, hi = slice(0, HALF), slice(HALF, T)
+        for t in range(PACK):
+            if t > 0:
+                scatter(t, slice(0, J))
+            nc.sync.dma_start(out=rows[t], in_=y[t][:])
+            if t < 2:
+                nc.scalar.copy(out=grouped[:, :, t], in_=y[t][:])
+            elif t == 2:
+                nc.scalar.copy(out=grouped[:, lo, 2:4], in_=y[t][:, lo].unsqueeze(2).to_broadcast([P, HALF, 2]))
+                nc.scalar.copy(out=grouped[:, hi, 2], in_=y[t][:, hi])
+            else:
+                nc.vector.tensor_copy(out=grouped[:, lo, t], in_=y[t][:, lo])
+                nc.scalar.copy(out=grouped[:, hi, t], in_=y[t][:, hi])
+        words = out_1[0].rearrange("p c r -> p (c r)").bitcast(I32)
+        for part in (lo, hi):
+            nc.vector.quantize_mx(out=yq[:, part].bitcast(FP8X4), scales=ys[:, part],
+                                  in_=grouped[:, part, :].rearrange("p c t -> p (c t)"))
+            nc.sync.dma_start(out=words[:, part], in_=yq[:, part])
+        for r in range(4):
+            queue = nc.scalar if r % 2 else nc.sync
+            queue.dma_start(out=out_2[0, r:16:4, :].bitcast(I32), in_=ys[r:P:32, :].bitcast(I32))

@@ -21,11 +21,12 @@ PACK = 4
 CHUNK = 128
 CHUNKS = J // CHUNK
 HALF = T // 2
+SPLIT = 640
 
 
-def load_scale_rows(nc, plane, scales):
-    for r in range(4):
-        nc.sync.dma_start(out=plane[r:P:32, :].bitcast(I32), in_=scales[0, r:16:4, :].bitcast(I32))
+def load_scale_rows(queue, plane, scales, rows=range(4)):
+    for r in rows:
+        queue.dma_start(out=plane[r:P:32, :].bitcast(I32), in_=scales[0, r:16:4, :].bitcast(I32))
 
 
 def deal_columns(nc, dealt, raw):
@@ -44,8 +45,8 @@ def tile_moe_expert_hidden_and_given_pl_kernel(
         keep = ctx.enter_context(tc.tile_pool(name="keep", bufs=1))
         psum = ctx.enter_context(tc.psum_pool(name="psum", bufs=1))
 
-        def sb(name, shape, dtype):
-            return keep.tile(shape, dtype, name=name, align_bytes=64)
+        def sb(name, shape, dtype, tag=None):
+            return keep.tile(shape, dtype, name=name, tag=tag or name, align_bytes=64)
 
         offsets = keep.tile([P, J // 16], U16, name="offsets")
         xw = sb("xw", [P, T], U16)
@@ -60,32 +61,37 @@ def tile_moe_expert_hidden_and_given_pl_kernel(
         sxs = sb("sxs", [P, J], U8)
         ga_cols = sb("ga_cols", [P, PACK], F32)
         ident = sb("ident", [P, P], F32)
-        y = [sb("y%d" % t, [P, T], F32) for t in range(PACK)]
 
-        for plane in (was, xs, wbs, wcs, sxs):
-            nc.vector.memset(plane[:].bitcast(I32), 0)
+        nc.gpsimd.memset(xs[:].bitcast(I32), 0)
         make_identity(nc, ident[:])
+        nc.gpsimd.memset(wcs[:].bitcast(I32), 0)
+        for plane in (was, wbs, sxs):
+            nc.vector.memset(plane[:].bitcast(I32), 0)
+        y = {t: sb("y%d" % t, [P, T], F32) for t in range(PACK)}
+        for t in (0, 2):
+            nc.vector.memset(y[t][:].bitcast(I32), 0)
 
         nc.sync.dma_start(offsets[:], offs)
         nc.sync.dma_start(out=xw[:].bitcast(I32), in_=xt_words[0].bitcast(I32))
+        load_scale_rows(nc.sync, xs, xt_scales)
         nc.sync.dma_start(out=waw[:], in_=wa_words[0].rearrange("p c r -> p (c r)").bitcast(I32))
-        load_scale_rows(nc, was, wa_scales)
         nc.sync.dma_start(out=ga_cols[:], in_=ga.rearrange("o (p c) -> p (o c)", c=PACK))
-        load_scale_rows(nc, xs, xt_scales)
+        load_scale_rows(nc.sync, was, wa_scales)
         nc.sync.dma_start(out=wbw[:].bitcast(I32), in_=wb_words[0].bitcast(I32))
-        load_scale_rows(nc, wbs, wb_scales)
         nc.sync.dma_start(out=wcw[:].bitcast(I32), in_=wc_words[0].bitcast(I32))
-        load_scale_rows(nc, wcs, wc_scales)
+        load_scale_rows(nc.sync, wcs, wc_scales, range(1))
+        load_scale_rows(nc.gpsimd, wcs, wc_scales, range(1, 4))
+        load_scale_rows(nc.sync, wbs, wb_scales)
         nc.sync.dma_start(out=sxw[:], in_=sx_words[0].rearrange("p c r -> p (c r)").bitcast(I32))
-        load_scale_rows(nc, sxs, sx_scales)
+        load_scale_rows(nc.sync, sxs, sx_scales)
+        for t in (1, 3):
+            nc.gpsimd.memset(y[t][:].bitcast(I32), 0)
 
         xgw = sb("xgw", [P, J], U16)
-        xgs = sb("xgs", [P, J], U8)
+        xgs = [sb("xgs0", [P, J // 2], U8)]
 
-        def gather(lo, hi):
-            lst = offsets[:, lo // 16 : hi // 16]
-            nc.vector.tensor_copy(out=xgw[:, lo:hi], in_=xw[:].indirect(lst))
-            nc.vector.tensor_copy(out=xgs[:, lo:hi], in_=xs[:].indirect(lst))
+        def gather_scales(h):
+            nc.vector.tensor_copy(out=xgs[h][:], in_=xs[:].indirect(offsets[:, h * 16 : (h + 1) * 16]))
 
         waw_d = sb("waw_d", [P, R], I32)
         was_d = sb("was_d", [P, R], U8)
@@ -94,17 +100,17 @@ def tile_moe_expert_hidden_and_given_pl_kernel(
         wcw_d = sb("wcw_d", [P, N], U16)
         wcs_d = sb("wcs_d", [P, N], U8)
 
-        gather(0, CHUNK)
+        nc.vector.tensor_copy(out=xgw[:], in_=xw[:].indirect(offsets[:]))
+        gather_scales(0)
         deal_columns(nc, waw_d[:], waw[:])
         deal_columns(nc, was_d[:], was[:])
-        gather(CHUNK, J)
+        xgs.append(sb("xgs1", [P, J // 2], U8, "was"))
+        gather_scales(1)
         deal_columns(nc, wbw_d[:], wbw[:])
-        deal_columns(nc, wbs_d[:], wbs[:])
         deal_columns(nc, wcw_d[:], wcw[:])
         deal_columns(nc, wcs_d[:], wcs[:])
+        deal_columns(nc, wbs_d[:], wbs[:])
 
-        for t in range(PACK):
-            (nc.vector if t < 2 else nc.gpsimd).memset(y[t][:], 0.0)
 
         ga_ps = psum.tile([P, PACK, P], F32, name="ga_ps", tag="full3")
         for c in range(PACK):
@@ -129,38 +135,42 @@ def tile_moe_expert_hidden_and_given_pl_kernel(
                                 rhs=hq[:, js].bitcast(FP8X4), rhs_scale=hs[:, js], start=first, stop=not first)
 
         def second_layer(bank, t, js):
-            hidden_pass(bank, t, js, True)
-            given_pass(bank, t, js, False)
+            given_pass(bank, t, js, True)
+            hidden_pass(bank, t, js, False)
 
         def scatter(t, js):
             nc.vector.tensor_tensor(y[t][:].indirect(offsets[:, js.start // 16 : js.stop // 16]), psb[t][:, js], ga_all[:, js], MULT)
 
         def first_layer(c):
-            a_ps = psum.tile([P, PACK, CHUNK], F32, name="a_ps", tag="a%d" % (c % 3))
+            a_ps = psum.tile([P, PACK, CHUNK], F32, name="a_ps", tag="a%d" % c)
             for t in range(PACK):
                 nc.tensor.matmul_mx(out=a_ps[:, t, :], lhsT=waw_d[:, cols(t)].bitcast(FP8X4), lhsT_scale=was_d[:, cols(t)],
-                                    rhs=xgw[:, cols(c)].bitcast(FP4X4), rhs_scale=xgs[:, cols(c)], start=True, stop=True)
+                                    rhs=xgw[:, cols(c)].bitcast(FP4X4), rhs_scale=xgs[c // 2][:, cols(c % 2)], start=True, stop=True)
             h = hid[:, c * CHUNK * PACK : (c + 1) * CHUNK * PACK]
             nc.scalar.activation(out=h.rearrange("p (j t) -> p j t", t=PACK), in_=a_ps[:].rearrange("p t j -> p j t"), func=RELU)
 
-        def quantize_hidden(c):
-            nc.vector.quantize_mx(out=hq[:, cols(c)].bitcast(FP8X4), scales=hs[:, cols(c)],
-                                  in_=hid[:, c * CHUNK * PACK : (c + 1) * CHUNK * PACK])
+        def quantize_hidden(chunks):
+            js = slice(chunks[0] * CHUNK, (chunks[-1] + 1) * CHUNK)
+            nc.vector.quantize_mx(out=hq[:, js].bitcast(FP8X4), scales=hs[:, js], in_=hid[:, js.start * PACK : js.stop * PACK])
 
-        def first_plane(c):
-            bank = psum.tile([P, CHUNK], F32, name="piece", tag="piece%d" % (c % 2))
-            second_layer(bank[:], 0, cols(c))
-            nc.scalar.copy(out=psb[0][:, cols(c)], in_=bank[:])
-            scatter(0, cols(c))
+        def first_plane(chunks, tag):
+            js = slice(chunks[0] * CHUNK, (chunks[-1] + 1) * CHUNK)
+            bank = psum.tile([P, len(chunks), CHUNK], F32, name="piece", tag=tag)
+            for i, c in enumerate(chunks):
+                second_layer(bank[:, i, :], 0, cols(c))
+            if chunks[0] == 0:
+                nc.vector.tensor_copy(out=psb[0][:, js], in_=bank[:].rearrange("p i j -> p (i j)"))
+            else:
+                nc.scalar.copy(out=psb[0][:, js], in_=bank[:].rearrange("p i j -> p (i j)"))
+            scatter(0, js)
 
-        first_layer(0)
-        for c in range(CHUNKS):
-            if c + 1 < CHUNKS:
-                first_layer(c + 1)
-            quantize_hidden(c)
-            if c > 0:
-                first_plane(c - 1)
-        first_plane(CHUNKS - 1)
+        for chunks in ([0], [1], [2, 3]):
+            for c in chunks:
+                first_layer(c)
+            quantize_hidden(chunks)
+        first_plane([0], "piece")
+        first_plane([1], "a0")
+        first_plane([2, 3], "a1")
         for t in range(1, PACK):
             bank = psum.tile([P, J], F32, name="full", tag="full%d" % t)
             second_layer(bank[:], t, slice(0, J))
@@ -170,7 +180,8 @@ def tile_moe_expert_hidden_and_given_pl_kernel(
         yq = sb("yq", [P, T], I32)
         ys = sb("ys", [P, T], U8)
         rows = out_0.rearrange("(p t) c -> t p c", t=PACK)
-        lo, hi = slice(0, HALF), slice(HALF, T)
+        lo = slice(0, HALF)
+        quarters = [slice(HALF, HALF + T // 4), slice(HALF + T // 4, T)]
         for t in range(PACK):
             if t > 0:
                 scatter(t, slice(0, J))
@@ -178,13 +189,15 @@ def tile_moe_expert_hidden_and_given_pl_kernel(
             if t < 2:
                 nc.scalar.copy(out=grouped[:, :, t], in_=y[t][:])
             elif t == 2:
-                nc.scalar.copy(out=grouped[:, lo, 2:4], in_=y[t][:, lo].unsqueeze(2).to_broadcast([P, HALF, 2]))
-                nc.scalar.copy(out=grouped[:, hi, 2], in_=y[t][:, hi])
+                nc.scalar.copy(out=grouped[:, 0:SPLIT, 2:4], in_=y[t][:, 0:SPLIT].unsqueeze(2).to_broadcast([P, SPLIT, 2]))
+                nc.scalar.copy(out=grouped[:, SPLIT:T, 2], in_=y[t][:, SPLIT:T])
             else:
-                nc.vector.tensor_copy(out=grouped[:, lo, t], in_=y[t][:, lo])
-                nc.scalar.copy(out=grouped[:, hi, t], in_=y[t][:, hi])
+                for part in (lo, slice(HALF, SPLIT)):
+                    nc.vector.tensor_copy(out=grouped[:, part, t], in_=y[t][:, part])
+                for part in (slice(SPLIT, quarters[0].stop), quarters[1]):
+                    nc.scalar.copy(out=grouped[:, part, t], in_=y[t][:, part])
         words = out_1[0].rearrange("p c r -> p (c r)").bitcast(I32)
-        for part in (lo, hi):
+        for part in [lo] + quarters:
             nc.vector.quantize_mx(out=yq[:, part].bitcast(FP8X4), scales=ys[:, part],
                                   in_=grouped[:, part, :].rearrange("p c t -> p (c t)"))
             nc.sync.dma_start(out=words[:, part], in_=yq[:, part])

@@ -64,12 +64,12 @@ def tile_moe_expert_hidden_and_given_pl_kernel(
 
         nc.gpsimd.memset(xs[:].bitcast(I32), 0)
         make_identity(nc, ident[:])
-        nc.gpsimd.memset(wcs[:].bitcast(I32), 0)
-        for plane in (was, wbs, sxs):
+        nc.gpsimd.memset(sxs[:].bitcast(I32), 0)
+        for plane in (was, wbs, wcs):
             nc.vector.memset(plane[:].bitcast(I32), 0)
-        y = {t: sb("y%d" % t, [P, T], F32) for t in range(PACK)}
-        for t in (0, 2):
-            nc.vector.memset(y[t][:].bitcast(I32), 0)
+        y = {t: sb("y%d" % t, [P, T], F32) for t in (0, 2, 3)}
+        for t in y:
+            (nc.gpsimd if t == 3 else nc.vector).memset(y[t][:].bitcast(I32), 0)
 
         nc.sync.dma_start(offsets[:], offs)
         nc.sync.dma_start(out=xw[:].bitcast(I32), in_=xt_words[0].bitcast(I32))
@@ -79,13 +79,10 @@ def tile_moe_expert_hidden_and_given_pl_kernel(
         load_scale_rows(nc.sync, was, wa_scales)
         nc.sync.dma_start(out=wbw[:].bitcast(I32), in_=wb_words[0].bitcast(I32))
         nc.sync.dma_start(out=wcw[:].bitcast(I32), in_=wc_words[0].bitcast(I32))
-        load_scale_rows(nc.sync, wcs, wc_scales, range(1))
-        load_scale_rows(nc.gpsimd, wcs, wc_scales, range(1, 4))
         load_scale_rows(nc.sync, wbs, wb_scales)
+        load_scale_rows(nc.sync, wcs, wc_scales)
         nc.sync.dma_start(out=sxw[:], in_=sx_words[0].rearrange("p c r -> p (c r)").bitcast(I32))
         load_scale_rows(nc.sync, sxs, sx_scales)
-        for t in (1, 3):
-            nc.gpsimd.memset(y[t][:].bitcast(I32), 0)
 
         xgw = sb("xgw", [P, J], U16)
         xgs = [sb("xgs0", [P, J // 2], U8)]
@@ -108,8 +105,10 @@ def tile_moe_expert_hidden_and_given_pl_kernel(
         gather_scales(1)
         deal_columns(nc, wbw_d[:], wbw[:])
         deal_columns(nc, wcw_d[:], wcw[:])
-        deal_columns(nc, wcs_d[:], wcs[:])
         deal_columns(nc, wbs_d[:], wbs[:])
+        deal_columns(nc, wcs_d[:], wcs[:])
+        y[1] = sb("y1", [P, T], F32, "wbw")
+        nc.vector.memset(y[1][:].bitcast(I32), 0)
 
 
         ga_ps = psum.tile([P, PACK, P], F32, name="ga_ps", tag="full3")

@@ -67,9 +67,9 @@ def tile_moe_expert_hidden_and_given_pl_kernel(
         nc.gpsimd.memset(sxs[:].bitcast(I32), 0)
         for plane in (was, wbs, wcs):
             nc.vector.memset(plane[:].bitcast(I32), 0)
-        y = {t: sb("y%d" % t, [P, T], F32) for t in (0, 2, 3)}
+        y = {t: sb("y%d" % t, [P, T], F32) for t in range(PACK)}
         for t in y:
-            (nc.gpsimd if t == 3 else nc.vector).memset(y[t][:].bitcast(I32), 0)
+            (nc.gpsimd if t % 2 else nc.vector).memset(y[t][:].bitcast(I32), 0)
 
         nc.sync.dma_start(offsets[:], offs)
         nc.sync.dma_start(out=xw[:].bitcast(I32), in_=xt_words[0].bitcast(I32))
@@ -79,9 +79,9 @@ def tile_moe_expert_hidden_and_given_pl_kernel(
         load_scale_rows(nc.sync, was, wa_scales)
         nc.sync.dma_start(out=wbw[:].bitcast(I32), in_=wb_words[0].bitcast(I32))
         nc.sync.dma_start(out=wcw[:].bitcast(I32), in_=wc_words[0].bitcast(I32))
+        nc.sync.dma_start(out=sxw[:], in_=sx_words[0].rearrange("p c r -> p (c r)").bitcast(I32))
         load_scale_rows(nc.sync, wbs, wb_scales)
         load_scale_rows(nc.sync, wcs, wc_scales)
-        nc.sync.dma_start(out=sxw[:], in_=sx_words[0].rearrange("p c r -> p (c r)").bitcast(I32))
         load_scale_rows(nc.sync, sxs, sx_scales)
 
         xgw = sb("xgw", [P, J], U16)
@@ -107,8 +107,6 @@ def tile_moe_expert_hidden_and_given_pl_kernel(
         deal_columns(nc, wcw_d[:], wcw[:])
         deal_columns(nc, wbs_d[:], wbs[:])
         deal_columns(nc, wcs_d[:], wcs[:])
-        y[1] = sb("y1", [P, T], F32, "wbw")
-        nc.vector.memset(y[1][:].bitcast(I32), 0)
 
 
         ga_ps = psum.tile([P, PACK, P], F32, name="ga_ps", tag="full3")
@@ -146,7 +144,11 @@ def tile_moe_expert_hidden_and_given_pl_kernel(
                 nc.tensor.matmul_mx(out=a_ps[:, t, :], lhsT=waw_d[:, cols(t)].bitcast(FP8X4), lhsT_scale=was_d[:, cols(t)],
                                     rhs=xgw[:, cols(c)].bitcast(FP4X4), rhs_scale=xgs[c // 2][:, cols(c % 2)], start=True, stop=True)
             h = hid[:, c * CHUNK * PACK : (c + 1) * CHUNK * PACK]
-            nc.scalar.activation(out=h.rearrange("p (j t) -> p j t", t=PACK), in_=a_ps[:].rearrange("p t j -> p j t"), func=RELU)
+            woven, sums = h.rearrange("p (j t) -> p j t", t=PACK), a_ps[:].rearrange("p t j -> p j t")
+            if c == 1:
+                nc.vector.tensor_scalar_max(woven, sums, 0.0)
+            else:
+                nc.scalar.activation(out=woven, in_=sums, func=RELU)
 
         def quantize_hidden(chunks):
             js = slice(chunks[0] * CHUNK, (chunks[-1] + 1) * CHUNK)
@@ -157,16 +159,12 @@ def tile_moe_expert_hidden_and_given_pl_kernel(
             bank = psum.tile([P, len(chunks), CHUNK], F32, name="piece", tag=tag)
             for i, c in enumerate(chunks):
                 second_layer(bank[:, i, :], 0, cols(c))
-            if chunks[0] == 0:
-                nc.vector.tensor_copy(out=psb[0][:, js], in_=bank[:].rearrange("p i j -> p (i j)"))
-            else:
-                nc.scalar.copy(out=psb[0][:, js], in_=bank[:].rearrange("p i j -> p (i j)"))
+            nc.scalar.copy(out=psb[0][:, js], in_=bank[:].rearrange("p i j -> p (i j)"))
             scatter(0, js)
 
-        for chunks in ([0], [1], [2, 3]):
-            for c in chunks:
-                first_layer(c)
-            quantize_hidden(chunks)
+        for c in range(CHUNKS):
+            first_layer(c)
+            quantize_hidden([c])
         first_plane([0], "piece")
         first_plane([1], "a0")
         first_plane([2, 3], "a1")

from contextlib import ExitStack

import concourse.mybir as mybir
from concourse.masks import make_identity

K, T, J, N, L, R = 512, 1024, 512, 512, 512, 512
FLOPS = 2 * J * (K * R + R * N + L * N)

F32 = mybir.dt.float32
BF16 = mybir.dt.bfloat16
I32 = mybir.dt.int32
U16 = mybir.dt.uint16
U8 = mybir.dt.uint8
FP8X4 = mybir.dt.float8_e4m3fn_x4
FP4X4 = mybir.dt.float4_e2m1fn_x4
RELU = mybir.ActivationFunctionType.Relu
MULT = mybir.AluOpType.mult

P = 128
PACK = 4
CHUNK = 128
CHUNKS = J // CHUNK
HALF = T // 2
SPLIT = 640


def load_scale_rows(queue, plane, scales, rows=range(4)):
    for r in rows:
        queue.dma_start(out=plane[r:P:32, :].bitcast(I32), in_=scales[0, r:16:4, :].bitcast(I32))


def deal_columns(nc, dealt, raw):
    nc.vector.tensor_copy(
        out=dealt.rearrange("p (t m) -> p t m", t=PACK),
        in_=raw.rearrange("p (m t) -> p t m", t=PACK),
    )


def tile_moe_expert_hidden_and_given_pl_kernel(
    tc, xt_words, xt_scales, wa_words, wa_scales, wb_words, wb_scales, sx_words, sx_scales, wc_words, wc_scales, ga, offs,
    out_0, out_1, out_2,
):
    nc = tc.nc
    with ExitStack() as ctx:
        keep = ctx.enter_context(tc.tile_pool(name="keep", bufs=1))
        psum = ctx.enter_context(tc.psum_pool(name="psum", bufs=1))

        def sb(name, shape, dtype, tag=None):
            return keep.tile(shape, dtype, name=name, tag=tag or name, align_bytes=64)

        offsets = keep.tile([P, J // 16], U16, name="offsets")
        xw = sb("xw", [P, T], U16)
        xs = sb("xs", [P, T], U8)
        waw = sb("waw", [P, R], I32)
        was = sb("was", [P, R], U8)
        wbw = sb("wbw", [P, N], U16)
        wbs = sb("wbs", [P, N], U8)
        wcw = sb("wcw", [P, N], U16)
        wcs = sb("wcs", [P, N], U8)
        sxw = sb("sxw", [P, J], I32)
        sxs = sb("sxs", [P, J], U8)
        ga_cols = sb("ga_cols", [P, PACK], F32)
        ident = sb("ident", [P, P], F32)

        nc.gpsimd.memset(xs[:].bitcast(I32), 0)
        make_identity(nc, ident[:])
        nc.gpsimd.memset(sxs[:].bitcast(I32), 0)
        for plane in (was, wbs, wcs):
            nc.vector.memset(plane[:].bitcast(I32), 0)
        y = {t: sb("y%d" % t, [P, T], F32) for t in range(PACK)}
        for t in y:
            (nc.gpsimd if t % 2 else nc.vector).memset(y[t][:].bitcast(I32), 0)

        nc.sync.dma_start(offsets[:], offs)
        nc.sync.dma_start(out=xw[:].bitcast(I32), in_=xt_words[0].bitcast(I32))
        load_scale_rows(nc.sync, xs, xt_scales)
        nc.sync.dma_start(out=waw[:], in_=wa_words[0].rearrange("p c r -> p (c r)").bitcast(I32))
        nc.sync.dma_start(out=ga_cols[:], in_=ga.rearrange("o (p c) -> p (o c)", c=PACK))
        load_scale_rows(nc.sync, was, wa_scales)
        nc.sync.dma_start(out=wbw[:].bitcast(I32), in_=wb_words[0].bitcast(I32))
        nc.sync.dma_start(out=wcw[:].bitcast(I32), in_=wc_words[0].bitcast(I32))
        nc.sync.dma_start(out=sxw[:], in_=sx_words[0].rearrange("p c r -> p (c r)").bitcast(I32))
        load_scale_rows(nc.sync, wbs, wb_scales)
        load_scale_rows(nc.sync, wcs, wc_scales)
        load_scale_rows(nc.sync, sxs, sx_scales)

        xgw = sb("xgw", [P, J], U16)
        xgs = [sb("xgs0", [P, J // 2], U8)]

        def gather_scales(h):
            nc.vector.tensor_copy(out=xgs[h][:], in_=xs[:].indirect(offsets[:, h * 16 : (h + 1) * 16]))

        waw_d = sb("waw_d", [P, R], I32)
        was_d = sb("was_d", [P, R], U8)
        wbw_d = sb("wbw_d", [P, N], U16)
        wbs_d = sb("wbs_d", [P, N], U8)
        wcw_d = sb("wcw_d", [P, N], U16)
        wcs_d = sb("wcs_d", [P, N], U8)

        nc.vector.tensor_copy(out=xgw[:], in_=xw[:].indirect(offsets[:]))
        gather_scales(0)
        deal_columns(nc, waw_d[:], waw[:])
        deal_columns(nc, was_d[:], was[:])
        xgs.append(sb("xgs1", [P, J // 2], U8, "was"))
        gather_scales(1)
        deal_columns(nc, wbw_d[:], wbw[:])
        deal_columns(nc, wcw_d[:], wcw[:])
        deal_columns(nc, wbs_d[:], wbs[:])
        deal_columns(nc, wcs_d[:], wcs[:])


        ga_ps = psum.tile([P, PACK, P], F32, name="ga_ps", tag="full3")
        for c in range(PACK):
            nc.tensor.transpose(ga_ps[:, c, :], ga_cols[:, c : c + 1].to_broadcast([P, P]), ident[:])
        ga_all = sb("ga_all", [P, J], F32)
        nc.scalar.copy(out=ga_all[:].rearrange("p (q c) -> p q c", c=PACK), in_=ga_ps[:].rearrange("p c q -> p q c"))

        hid = sb("hid", [P, J * PACK], BF16)
        hq = sb("hq", [P, J], I32)
        hs = sb("hs", [P, J], U8)
        psb = [sb("psb%d" % t, [P, J], F32) for t in range(PACK)]

        def cols(i):
            return slice(i * P, (i + 1) * P)

        def given_pass(bank, t, js, first):
            nc.tensor.matmul_mx(out=bank, lhsT=wcw_d[:, cols(t)].bitcast(FP4X4), lhsT_scale=wcs_d[:, cols(t)],
                                rhs=sxw[:, js].bitcast(FP8X4), rhs_scale=sxs[:, js], start=first, stop=not first)

        def hidden_pass(bank, t, js, first):
            nc.tensor.matmul_mx(out=bank, lhsT=wbw_d[:, cols(t)].bitcast(FP4X4), lhsT_scale=wbs_d[:, cols(t)],
                                rhs=hq[:, js].bitcast(FP8X4), rhs_scale=hs[:, js], start=first, stop=not first)

        def second_layer(bank, t, js):
            given_pass(bank, t, js, True)
            hidden_pass(bank, t, js, False)

        def scatter(t, js):
            nc.vector.tensor_tensor(y[t][:].indirect(offsets[:, js.start // 16 : js.stop // 16]), psb[t][:, js], ga_all[:, js], MULT)

        def first_layer(c):
            a_ps = psum.tile([P, PACK, CHUNK], F32, name="a_ps", tag="a%d" % c)
            for t in range(PACK):
                nc.tensor.matmul_mx(out=a_ps[:, t, :], lhsT=waw_d[:, cols(t)].bitcast(FP8X4), lhsT_scale=was_d[:, cols(t)],
                                    rhs=xgw[:, cols(c)].bitcast(FP4X4), rhs_scale=xgs[c // 2][:, cols(c % 2)], start=True, stop=True)
            h = hid[:, c * CHUNK * PACK : (c + 1) * CHUNK * PACK]
            woven, sums = h.rearrange("p (j t) -> p j t", t=PACK), a_ps[:].rearrange("p t j -> p j t")
            if c == 1:
                nc.vector.tensor_scalar_max(woven, sums, 0.0)
            else:
                nc.scalar.activation(out=woven, in_=sums, func=RELU)

        def quantize_hidden(chunks):
            js = slice(chunks[0] * CHUNK, (chunks[-1] + 1) * CHUNK)
            nc.vector.quantize_mx(out=hq[:, js].bitcast(FP8X4), scales=hs[:, js], in_=hid[:, js.start * PACK : js.stop * PACK])

        def first_plane(chunks, tag):
            js = slice(chunks[0] * CHUNK, (chunks[-1] + 1) * CHUNK)
            bank = psum.tile([P, len(chunks), CHUNK], F32, name="piece", tag=tag)
            for i, c in enumerate(chunks):
                second_layer(bank[:, i, :], 0, cols(c))
            nc.scalar.copy(out=psb[0][:, js], in_=bank[:].rearrange("p i j -> p (i j)"))
            scatter(0, js)

        for c in range(CHUNKS):
            first_layer(c)
            quantize_hidden([c])
        first_plane([0], "piece")
        first_plane([1], "a0")
        first_plane([2, 3], "a1")
        for t in range(1, PACK):
            bank = psum.tile([P, J], F32, name="full", tag="full%d" % t)
            second_layer(bank[:], t, slice(0, J))
            nc.scalar.copy(out=psb[t][:], in_=bank[:])

        grouped = sb("grouped", [P, T, PACK], BF16)
        yq = sb("yq", [P, T], I32)
        ys = sb("ys", [P, T], U8)
        rows = out_0.rearrange("(p t) c -> t p c", t=PACK)
        lo = slice(0, HALF)
        quarters = [slice(HALF, HALF + T // 4), slice(HALF + T // 4, T)]
        for t in range(PACK):
            if t > 0:
                scatter(t, slice(0, J))
            nc.sync.dma_start(out=rows[t], in_=y[t][:])
            if t < 2:
                nc.scalar.copy(out=grouped[:, :, t], in_=y[t][:])
            elif t == 2:
                nc.scalar.copy(out=grouped[:, 0:SPLIT, 2:4], in_=y[t][:, 0:SPLIT].unsqueeze(2).to_broadcast([P, SPLIT, 2]))
                nc.scalar.copy(out=grouped[:, SPLIT:T, 2], in_=y[t][:, SPLIT:T])
            else:
                for part in (lo, slice(HALF, SPLIT)):
                    nc.vector.tensor_copy(out=grouped[:, part, t], in_=y[t][:, part])
                for part in (slice(SPLIT, quarters[0].stop), quarters[1]):
                    nc.scalar.copy(out=grouped[:, part, t], in_=y[t][:, part])
        words = out_1[0].rearrange("p c r -> p (c r)").bitcast(I32)
        for part in [lo] + quarters:
            nc.vector.quantize_mx(out=yq[:, part].bitcast(FP8X4), scales=ys[:, part],
                                  in_=grouped[:, part, :].rearrange("p c t -> p (c t)"))
            nc.sync.dma_start(out=words[:, part], in_=yq[:, part])
        for r in range(4):
            queue = nc.scalar if r % 2 else nc.sync
            queue.dma_start(out=out_2[0, r:16:4, :].bitcast(I32), in_=ys[r:P:32, :].bitcast(I32))
